import numpy as np, ml_dtypes
CORES = [35,38,43,46]
N = 4
import mx_ref
NC, G = 512, 4
C = np.float32(0.047)
BF = ml_dtypes.bfloat16
def cut(t, i, w=512):
    return t[:, w * i:w * i + w]
def tile(rs):
    return np.stack(rs, axis=2).reshape(128, -1).astype(BF)
def layer(w, X):
    out = []
    for i in range(G):
        for t in range(len(X)):
            p = mx_ref.matmul(mx_ref.quantize(cut(w, len(X) * i + t)), X[t])
            z = p if t == 0 else z + p
        out.append(z)
    return out
def setup_inputs(rng):
    def f(*shape):
        return mx_ref.flush((rng.standard_normal(shape, dtype=np.float32) * np.exp2(rng.integers(-2, 3, shape[:-1] + (1,)))).astype(BF))
    return {"x": f(N, 128, 4 * NC), "w": f(N, 128, 512), "a": np.broadcast_to(f(1, 128, 4 * 512), (N, 128, 4 * 512)).copy(), "bb": f(N, 128, 512)}
def setup_inputs_blocks(rng):
    d = setup_inputs(rng)
    for k in ("x", "w", "bb"): d[k] = mx_ref.spread(d[k], rng, 4)
    return d
def setup_inputs_wide(rng):
    d = setup_inputs(rng)
    for k in ("x", "w", "bb"): d[k] = mx_ref.flush((d[k].astype(np.float32) * np.exp2(rng.integers(-6, 7, (N, 1, 1))).astype(np.float32)).astype(BF))
    return d
def setup_inputs_zeros(rng):
    d = setup_inputs(rng); v = d["x"].reshape(N, 128, -1, 4).copy()
    v[np.broadcast_to((rng.random((N, 1, v.shape[2], 1)) < 0.33), v.shape)] = 0
    d["x"] = v.reshape(d["x"].shape)
    return d
def reference(x, w, a, bb):
    X = [mx_ref.quantize(x[j]) for j in range(N)]
    T = [mx_ref.quantize(tile([z * C for z in layer(a[j], [X[j]])])) for j in range(N)]
    y = np.zeros((N, 128, N * NC), np.float32)
    for r in range(N):
        qw = mx_ref.quantize(w[r]); qb = mx_ref.quantize(bb[r])
        for j in range(N):
            y[r][:, NC * j:NC * j + NC] = mx_ref.matmul(qw, X[j]) + mx_ref.matmul(qb, T[j])
    return {"y": y}

@@ -1,0 +1,254 @@
+from concourse.bass import DstId, RemoteDMATransfer
+from concourse.mybir import dt, AluOpType, ActivationFunctionType
+
+N, NC, G, SCALE = 4, 512, 4, 0.047
+CH = [(0, 256), (256, 512)]
+NCH = len(CH)
+ZBANKS, YBANKS = 6, 2
+ALOAD = 2
+S_STEADY = (0, 1, 2)
+S_LAST = (0, 1)
+S_OWN = (0, 1, 2)
+
+SCRATCH = {
+    "xb": ("sbuf", [128, 4 * NC], "bfloat16"),
+    "ab": ("sbuf", [128, 4 * 512], "bfloat16"),
+    "wb": ("sbuf", [128, 512], "bfloat16"),
+    "bf": ("sbuf", [128, 512], "bfloat16"),
+    "aq": ("sbuf", [128, 512], "float8_e4m3fn_x4"),
+    "az": ("sbuf", [128, 512], "uint8"),
+    "wq": ("sbuf", [128, 128], "float8_e4m3fn_x4"),
+    "wz": ("sbuf", [128, 128], "uint8"),
+    "bq": ("sbuf", [128, 128], "float8_e4m3fn_x4"),
+    "bz": ("sbuf", [128, 128], "uint8"),
+    "yb": ("sbuf", [128, N * NC], "float32"),
+    "ps": ("psum", [128, 4096], "float32"),
+}
+for _j in range(N):
+    SCRATCH["xq%d" % _j] = ("sbuf", [128, NC], "float8_e4m3fn_x4")
+    SCRATCH["xz%d" % _j] = ("sbuf", [128, NC], "uint8")
+    SCRATCH["tq%d" % _j] = ("sbuf", [128, NC], "float8_e4m3fn_x4")
+    SCRATCH["tz%d" % _j] = ("sbuf", [128, NC], "uint8")
+    SCRATCH["tb%d" % _j] = ("sbuf", [128, 4 * NC], "bfloat16")
+SEMAPHORES = ["lw", "lb", "qw", "qb", "st", "sent"]
+for _c in range(NCH):
+    SEMAPHORES += ["lx%d" % _c, "qx%d" % _c]
+    for _j in range(N):
+        SEMAPHORES += ["ax%d_%d" % (_j, _c), "at%d_%d" % (_j, _c), "qt%d_%d" % (_j, _c), "py%d_%d" % (_j, _c), "cy%d_%d" % (_j, _c)]
+        for _b in range(G):
+            SEMAPHORES += ["pz%d_%d_%d" % (_j, _c, _b), "sz%d_%d_%d" % (_j, _c, _b)]
+for _i in range(4):
+    SEMAPHORES += ["la%d" % _i, "qa%d" % _i]
+
+
+def count(mask):
+    return bin(mask).count("1")
+
+
+def rank_program(g, core, T, topo):
+    me = T.rank_of(core)
+    if me is None:
+        return
+    here = topo.chip(core)
+    others = [j for j in range(N) if j != me]
+    partner = [j for j in others if topo.chip(T.cores[j]) == here][0]
+    mates = [j for j in others if topo.mates(topo.chip(T.cores[j]), here)]
+    mates.sort(key=lambda j: topo.die(T.cores[j]) != topo.die(core))
+    moff = topo.mask(core, T.cores[mates[0]])
+    mon = topo.mask(core, T.cores[partner])
+    mon_hi = mon & ~moff
+
+    seen = set()
+
+    def wait(q, qn, ev, n):
+        if (qn, ev) not in seen:
+            seen.add((qn, ev))
+            q.wait_ge(T.sem[ev], n)
+
+    def sl(name, lo, hi):
+        return T[name][:, lo:hi]
+
+    def codes(name, lo, hi):
+        return T[name][:, lo:hi].bitcast(dt.uint8)
+
+    def dst(j):
+        a = topo.addr(T.cores[j])
+        return DstId(rid=a[0], pnc=a[1])
+
+    ins = {"x": T.x, "a": T.a}
+    lq = [g.sync, g.scalar]
+    k = 0
+    for c, (lo, hi) in enumerate(CH):
+        lq[k % 2].dma_start(sl("xb", 4 * lo, 4 * hi), T.x[:, 4 * lo:4 * hi]).then_inc(T.sem["lx%d" % c], 16)
+        k += 1
+    w = 2048 // ALOAD
+    for i in range(ALOAD):
+        lq[k % 2].dma_start(sl("ab", w * i, w * i + w), T.a[:, w * i:w * i + w]).then_inc(T.sem["la%d" % i], 16)
+        k += 1
+    lq[k % 2].dma_start(T.wb[:], T.w[:]).then_inc(T.sem.lw, 16)
+    lq[(k + 1) % 2].dma_start(T.bf[:], T.bb[:]).then_inc(T.sem.lb, 16)
+
+    own = [(me, c) for c in range(NCH)]
+    rem = [(m, c) for c in range(NCH) for m in mates]
+    pun = [(partner, c) for c in range(NCH)]
+    units = own + rem
+    last = units[-1]
+
+    def tag(u):
+        return "%d_%d" % u
+
+    def sset(u):
+        return S_LAST if u == last else S_OWN if u in own else S_STEADY
+
+    def border(u):
+        s = [b for b in range(G) if b in sset(u)]
+        v = [b for b in range(G) if b not in sset(u)]
+        o = []
+        while s or v:
+            if s:
+                o.append(s.pop(0))
+            if v:
+                o.append(v.pop(0))
+        return o
+
+    pe = g.tensor
+    bank_of, rel = {}, {}
+    zi, yi = [0], [0]
+
+    def xwait(u):
+        if u[0] == me:
+            wait(pe, "pe", "qx%d" % u[1], 1)
+        elif u[0] in mates:
+            wait(pe, "pe", "ax" + tag(u), 2 * count(moff))
+        else:
+            wait(pe, "pe", "ax" + tag(u), 2 * count(mon_hi))
+
+    def drained(bank):
+        if bank in rel:
+            wait(pe, "pe", rel[bank], 1)
+
+    def Z(u):
+        lo, hi = CH[u[1]]
+        for b in border(u):
+            bank = zi[0] % ZBANKS
+            zi[0] += 1
+            drained(bank)
+            xwait(u)
+            wait(pe, "pe", "qa%d" % b, 1)
+            pe.matmul_mx(sl("ps", 512 * bank, 512 * bank + hi - lo), sl("aq", 128 * b, 128 * b + 128), sl("az", 128 * b, 128 * b + 128),
+                         sl("xq%d" % u[0], lo, hi), sl("xz%d" % u[0], lo, hi), True, True).then_inc(T.sem["pz%s_%d" % (tag(u), b)], 1)
+            rel[bank] = "sz%s_%d" % (tag(u), b)
+            bank_of[u, b] = bank
+
+    def Y(u):
+        lo, hi = CH[u[1]]
+        bank = ZBANKS + yi[0] % YBANKS
+        yi[0] += 1
+        drained(bank)
+        xwait(u)
+        wait(pe, "pe", "qw", 1)
+        o = sl("ps", 512 * bank, 512 * bank + hi - lo)
+        pe.matmul_mx(o, T.wq[:], T.wz[:], sl("xq%d" % u[0], lo, hi), sl("xz%d" % u[0], lo, hi), True, False)
+        wait(pe, "pe", "qb", 1)
+        if u[0] == partner:
+            wait(pe, "pe", "at" + tag(u), 2 * count(mon_hi))
+        else:
+            wait(pe, "pe", "qt" + tag(u), 1)
+        pe.matmul_mx(o, T.bq[:], T.bz[:], sl("tq%d" % u[0], lo, hi), sl("tz%d" % u[0], lo, hi), False, True).then_inc(T.sem["py" + tag(u)], 1)
+        rel[bank] = "cy" + tag(u)
+        bank_of[u] = bank
+
+    for u in own:
+        Z(u)
+    for u in own:
+        Y(u)
+    for i, u in enumerate(rem):
+        Z(u)
+        if i > 0:
+            Y(rem[i - 1])
+    for u in pun:
+        Y(u)
+    Y(last)
+
+    def scale(qn, u, b):
+        q = g.scalar if qn == "s" else g.vector
+        lo, hi = CH[u[1]]
+        bank = bank_of[u, b]
+        wait(q, qn, "pz%s_%d" % (tag(u), b), 1)
+        o = T["tb%d" % u[0]][:, 4 * lo + b:4 * hi:4]
+        i = sl("ps", 512 * bank, 512 * bank + hi - lo)
+        if qn == "s":
+            r = q.activation(o, i, ActivationFunctionType.Copy, scale=SCALE)
+        else:
+            r = q.tensor_scalar(o, i, SCALE, None, AluOpType.mult)
+        r.then_inc(T.sem["sz%s_%d" % (tag(u), b)], 1)
+
+    def ycopy(qn, u):
+        q = g.scalar if qn == "s" else g.vector
+        lo, hi = CH[u[1]]
+        bank = bank_of[u]
+        wait(q, qn, "py" + tag(u), 1)
+        o = sl("yb", NC * u[0] + lo, NC * u[0] + hi)
+        i = sl("ps", 512 * bank, 512 * bank + hi - lo)
+        r = q.activation(o, i, ActivationFunctionType.Copy) if qn == "s" else q.tensor_copy(o, i)
+        r.then_inc(T.sem["cy" + tag(u)], 1)
+
+    def quant(u):
+        lo, hi = CH[u[1]]
+        for b in range(G):
+            wait(g.vector, "v", "sz%s_%d" % (tag(u), b), 1)
+        g.vector.quantize_mx(sl("tq%d" % u[0], lo, hi), sl("tz%d" % u[0], lo, hi), sl("tb%d" % u[0], 4 * lo, 4 * hi)).then_inc(T.sem["qt" + tag(u)], 1)
+
+    v = g.vector
+    for c, (lo, hi) in enumerate(CH):
+        wait(v, "v", "lx%d" % c, 16)
+        v.quantize_mx(sl("xq%d" % me, lo, hi), sl("xz%d" % me, lo, hi), sl("xb", 4 * lo, 4 * hi)).then_inc(T.sem["qx%d" % c], 1)
+    for i in range(G):
+        wait(v, "v", "la%d" % (i * ALOAD // 4), 16)
+        v.quantize_mx(sl("aq", 128 * i, 128 * i + 128), sl("az", 128 * i, 128 * i + 128), sl("ab", 512 * i, 512 * i + 512)).then_inc(T.sem["qa%d" % i], 1)
+
+    for i, u in enumerate(units):
+        for b in border(u):
+            if b not in sset(u):
+                scale("v", u, b)
+        if i == 0:
+            for nm, src, ld in (("w", "wb", "lw"), ("b", "bf", "lb")):
+                wait(v, "v", ld, 16)
+                v.quantize_mx(T[nm + "q"][:], T[nm + "z"][:], T[src][:]).then_inc(T.sem["q" + nm], 1)
+        if i > 0 and units[i - 1] != own[-1]:
+            ycopy("v", units[i - 1])
+        quant(u)
+        if u == own[-1]:
+            ycopy("v", u)
+    ycopy("v", last)
+    for u in units:
+        for b in border(u):
+            if b in sset(u):
+                scale("s", u, b)
+    for u in pun:
+        ycopy("s", u)
+
+    n = 0
+    for u in units[:-1] + pun + [last]:
+        lo, hi = CH[u[1]]
+        wait(g.sync, "y", "cy" + tag(u), 1)
+        g.sync.dma_start(T.y[:, NC * u[0] + lo:NC * u[0] + hi], sl("yb", NC * u[0] + lo, NC * u[0] + hi)).then_inc(T.sem.st, 16)
+        n += 16
+    g.sync.wait_ge(T.sem.st, n)
+
+    tot = 0
+    for c, (lo, hi) in enumerate(CH):
+        wait(g, "g", "qx%d" % c, 1)
+        for f in (codes("xq%d" % me, lo, hi), sl("xz%d" % me, lo, hi)):
+            g.remote_dma_fused([RemoteDMATransfer(dst_ids=[dst(m) for m in mates], dma_engine_mask=moff, remote_sem=T.sem["ax%d_%d" % (me, c)],
+                                                  srcs=[f], dsts=[f for m in mates]),
+                                RemoteDMATransfer(dst_ids=[dst(partner)], dma_engine_mask=mon_hi, remote_sem=T.sem["ax%d_%d" % (me, c)],
+                                                  srcs=[f], dsts=[f])], local_sem=T.sem.sent)
+            tot += count(moff) + count(mon_hi)
+    for c, (lo, hi) in enumerate(CH):
+        wait(g, "g", "qt%d_%d" % (me, c), 1)
+        for f in (codes("tq%d" % me, lo, hi), sl("tz%d" % me, lo, hi)):
+            g.remote_dma_fused([RemoteDMATransfer(dst_ids=[dst(partner)], dma_engine_mask=mon_hi, remote_sem=T.sem["at%d_%d" % (me, c)], srcs=[f], dsts=[f])],
+                               local_sem=T.sem.sent)
+            tot += count(mon_hi)
+    g.wait_ge(T.sem.sent, tot)

@@ -4,11 +4,18 @@ from concourse.mybir import dt, AluOpType, ActivationFunctionType
 N, NC, G, SCALE = 4, 512, 4, 0.047
 CH = [(0, 256), (256, 512)]
 NCH = len(CH)
-ZBANKS, YBANKS = 6, 2
 ALOAD = 2
-S_STEADY = (0, 1, 2)
-S_LAST = (0, 1)
-S_OWN = (0, 1, 2)
+XORDER = [0, 1]
+AORDER = [0, 2, 1, 3]
+SEND = ["m1", "n1", "p0", "p1"]
+RELAY = ["x1"]
+GQ = ["x0", "x1", "t1", "t0", "rx1"]
+PE = "Zo1 Zo0 Yo1 Yo0 Zm0 Zn0 Yp1 Ym0 Yn0 Yp0 Ym1 Yn1".split()
+VQ = "To1 W Qo1 To0 Yo1 Qo0 Yo0 Tm0 Qm0 Tn0 Qn0 Yp1 Yn0 Ym1".split()
+SQ = "To1 To0 Tm0 Tn0 Ym0 Yp0 Yn1".split()
+ST = "o1 o0 m0 p1 n0 p0 m1 n1".split()
+SSET = {"o1": (0, 1, 2), "o0": (0, 1), "m0": (0, 1), "n0": (0, 1)}
+BANKS = 8
 
 SCRATCH = {
     "xb": ("sbuf", [128, 4 * NC], "bfloat16"),
@@ -22,7 +29,7 @@ SCRATCH = {
     "bq": ("sbuf", [128, 128], "float8_e4m3fn_x4"),
     "bz": ("sbuf", [128, 128], "uint8"),
     "yb": ("sbuf", [128, N * NC], "float32"),
-    "ps": ("psum", [128, 4096], "float32"),
+    "ps": ("psum", [128, 512 * BANKS], "float32"),
 }
 for _j in range(N):
     SCRATCH["xq%d" % _j] = ("sbuf", [128, NC], "float8_e4m3fn_x4")
@@ -54,9 +61,9 @@ def rank_program(g, core, T, topo):
     partner = [j for j in others if topo.chip(T.cores[j]) == here][0]
     mates = [j for j in others if topo.mates(topo.chip(T.cores[j]), here)]
     mates.sort(key=lambda j: topo.die(T.cores[j]) != topo.die(core))
+    role = {"o": me, "p": partner, "m": mates[0], "n": mates[1]}
     moff = topo.mask(core, T.cores[mates[0]])
-    mon = topo.mask(core, T.cores[partner])
-    mon_hi = mon & ~moff
+    mon_hi = topo.mask(core, T.cores[partner]) & ~moff
 
     seen = set()
 
@@ -75,10 +82,31 @@ def rank_program(g, core, T, topo):
         a = topo.addr(T.cores[j])
         return DstId(rid=a[0], pnc=a[1])
 
-    ins = {"x": T.x, "a": T.a}
+    def unit(s):
+        return role[s[-2]], int(s[-1]), s[-2:]
+
+    def tag(u):
+        return "%d_%d" % u[:2]
+
+    def landed(nm, u):
+        relayed = u[2][0] == "n" and "%s%d" % (nm, u[1]) in RELAY
+        return 2 * count(mon_hi if u[0] == partner or relayed else moff)
+
+    def border(u):
+        s = [b for b in range(G) if b in SSET[u[2]]]
+        v = [b for b in range(G) if b not in SSET[u[2]]]
+        o = []
+        while s or v:
+            if s:
+                o.append(s.pop(0))
+            if v:
+                o.append(v.pop(0))
+        return o
+
     lq = [g.sync, g.scalar]
     k = 0
-    for c, (lo, hi) in enumerate(CH):
+    for c in XORDER:
+        lo, hi = CH[c]
         lq[k % 2].dma_start(sl("xb", 4 * lo, 4 * hi), T.x[:, 4 * lo:4 * hi]).then_inc(T.sem["lx%d" % c], 16)
         k += 1
     w = 2048 // ALOAD
@@ -88,95 +116,58 @@ def rank_program(g, core, T, topo):
     lq[k % 2].dma_start(T.wb[:], T.w[:]).then_inc(T.sem.lw, 16)
     lq[(k + 1) % 2].dma_start(T.bf[:], T.bb[:]).then_inc(T.sem.lb, 16)
 
-    own = [(me, c) for c in range(NCH)]
-    rem = [(m, c) for c in range(NCH) for m in mates]
-    pun = [(partner, c) for c in range(NCH)]
-    units = own + rem
-    last = units[-1]
-
-    def tag(u):
-        return "%d_%d" % u
-
-    def sset(u):
-        return S_LAST if u == last else S_OWN if u in own else S_STEADY
-
-    def border(u):
-        s = [b for b in range(G) if b in sset(u)]
-        v = [b for b in range(G) if b not in sset(u)]
-        o = []
-        while s or v:
-            if s:
-                o.append(s.pop(0))
-            if v:
-                o.append(v.pop(0))
-        return o
-
     pe = g.tensor
     bank_of, rel = {}, {}
-    zi, yi = [0], [0]
+    turn = [0]
+
+    def bank():
+        b = turn[0] % BANKS
+        turn[0] += 1
+        if b in rel:
+            wait(pe, "pe", rel[b], 1)
+        return b
 
     def xwait(u):
         if u[0] == me:
             wait(pe, "pe", "qx%d" % u[1], 1)
-        elif u[0] in mates:
-            wait(pe, "pe", "ax" + tag(u), 2 * count(moff))
         else:
-            wait(pe, "pe", "ax" + tag(u), 2 * count(mon_hi))
+            wait(pe, "pe", "ax" + tag(u), landed("x", u))
 
-    def drained(bank):
-        if bank in rel:
-            wait(pe, "pe", rel[bank], 1)
-
-    def Z(u):
+    for s in PE:
+        u = unit(s)
         lo, hi = CH[u[1]]
-        for b in border(u):
-            bank = zi[0] % ZBANKS
-            zi[0] += 1
-            drained(bank)
+        x, xz = sl("xq%d" % u[0], lo, hi), sl("xz%d" % u[0], lo, hi)
+        if s[0] == "Z":
+            for b in border(u):
+                k = bank()
+                xwait(u)
+                wait(pe, "pe", "qa%d" % b, 1)
+                pe.matmul_mx(sl("ps", 512 * k, 512 * k + hi - lo), sl("aq", 128 * b, 128 * b + 128), sl("az", 128 * b, 128 * b + 128),
+                             x, xz, True, True).then_inc(T.sem["pz%s_%d" % (tag(u), b)], 1)
+                rel[k] = "sz%s_%d" % (tag(u), b)
+                bank_of[u, b] = k
+        else:
+            k = bank()
             xwait(u)
-            wait(pe, "pe", "qa%d" % b, 1)
-            pe.matmul_mx(sl("ps", 512 * bank, 512 * bank + hi - lo), sl("aq", 128 * b, 128 * b + 128), sl("az", 128 * b, 128 * b + 128),
-                         sl("xq%d" % u[0], lo, hi), sl("xz%d" % u[0], lo, hi), True, True).then_inc(T.sem["pz%s_%d" % (tag(u), b)], 1)
-            rel[bank] = "sz%s_%d" % (tag(u), b)
-            bank_of[u, b] = bank
-
-    def Y(u):
-        lo, hi = CH[u[1]]
-        bank = ZBANKS + yi[0] % YBANKS
-        yi[0] += 1
-        drained(bank)
-        xwait(u)
-        wait(pe, "pe", "qw", 1)
-        o = sl("ps", 512 * bank, 512 * bank + hi - lo)
-        pe.matmul_mx(o, T.wq[:], T.wz[:], sl("xq%d" % u[0], lo, hi), sl("xz%d" % u[0], lo, hi), True, False)
-        wait(pe, "pe", "qb", 1)
-        if u[0] == partner:
-            wait(pe, "pe", "at" + tag(u), 2 * count(mon_hi))
-        else:
-            wait(pe, "pe", "qt" + tag(u), 1)
-        pe.matmul_mx(o, T.bq[:], T.bz[:], sl("tq%d" % u[0], lo, hi), sl("tz%d" % u[0], lo, hi), False, True).then_inc(T.sem["py" + tag(u)], 1)
-        rel[bank] = "cy" + tag(u)
-        bank_of[u] = bank
-
-    for u in own:
-        Z(u)
-    for u in own:
-        Y(u)
-    for i, u in enumerate(rem):
-        Z(u)
-        if i > 0:
-            Y(rem[i - 1])
-    for u in pun:
-        Y(u)
-    Y(last)
+            wait(pe, "pe", "qw", 1)
+            o = sl("ps", 512 * k, 512 * k + hi - lo)
+            pe.matmul_mx(o, T.wq[:], T.wz[:], x, xz, True, False)
+            wait(pe, "pe", "qb", 1)
+            if u[2] in SEND:
+                wait(pe, "pe", "at" + tag(u), landed("t", u))
+            else:
+                wait(pe, "pe", "qt" + tag(u), 1)
+            pe.matmul_mx(o, T.bq[:], T.bz[:], sl("tq%d" % u[0], lo, hi), sl("tz%d" % u[0], lo, hi), False, True).then_inc(T.sem["py" + tag(u)], 1)
+            rel[k] = "cy" + tag(u)
+            bank_of[u] = k
 
     def scale(qn, u, b):
         q = g.scalar if qn == "s" else g.vector
         lo, hi = CH[u[1]]
-        bank = bank_of[u, b]
+        k = bank_of[u, b]
         wait(q, qn, "pz%s_%d" % (tag(u), b), 1)
         o = T["tb%d" % u[0]][:, 4 * lo + b:4 * hi:4]
-        i = sl("ps", 512 * bank, 512 * bank + hi - lo)
+        i = sl("ps", 512 * k, 512 * k + hi - lo)
         if qn == "s":
             r = q.activation(o, i, ActivationFunctionType.Copy, scale=SCALE)
         else:
@@ -186,69 +177,78 @@ def rank_program(g, core, T, topo):
     def ycopy(qn, u):
         q = g.scalar if qn == "s" else g.vector
         lo, hi = CH[u[1]]
-        bank = bank_of[u]
+        k = bank_of[u]
         wait(q, qn, "py" + tag(u), 1)
         o = sl("yb", NC * u[0] + lo, NC * u[0] + hi)
-        i = sl("ps", 512 * bank, 512 * bank + hi - lo)
+        i = sl("ps", 512 * k, 512 * k + hi - lo)
         r = q.activation(o, i, ActivationFunctionType.Copy) if qn == "s" else q.tensor_copy(o, i)
         r.then_inc(T.sem["cy" + tag(u)], 1)
 
-    def quant(u):
-        lo, hi = CH[u[1]]
-        for b in range(G):
-            wait(g.vector, "v", "sz%s_%d" % (tag(u), b), 1)
-        g.vector.quantize_mx(sl("tq%d" % u[0], lo, hi), sl("tz%d" % u[0], lo, hi), sl("tb%d" % u[0], 4 * lo, 4 * hi)).then_inc(T.sem["qt" + tag(u)], 1)
-
     v = g.vector
-    for c, (lo, hi) in enumerate(CH):
+    for c in XORDER:
+        lo, hi = CH[c]
         wait(v, "v", "lx%d" % c, 16)
         v.quantize_mx(sl("xq%d" % me, lo, hi), sl("xz%d" % me, lo, hi), sl("xb", 4 * lo, 4 * hi)).then_inc(T.sem["qx%d" % c], 1)
-    for i in range(G):
+    for i in border(unit(PE[0])):
         wait(v, "v", "la%d" % (i * ALOAD // 4), 16)
         v.quantize_mx(sl("aq", 128 * i, 128 * i + 128), sl("az", 128 * i, 128 * i + 128), sl("ab", 512 * i, 512 * i + 512)).then_inc(T.sem["qa%d" % i], 1)
 
-    for i, u in enumerate(units):
-        for b in border(u):
-            if b not in sset(u):
-                scale("v", u, b)
-        if i == 0:
+    for s in VQ:
+        if s == "W":
             for nm, src, ld in (("w", "wb", "lw"), ("b", "bf", "lb")):
                 wait(v, "v", ld, 16)
                 v.quantize_mx(T[nm + "q"][:], T[nm + "z"][:], T[src][:]).then_inc(T.sem["q" + nm], 1)
-        if i > 0 and units[i - 1] != own[-1]:
-            ycopy("v", units[i - 1])
-        quant(u)
-        if u == own[-1]:
+            continue
+        u = unit(s)
+        if s[0] == "T":
+            for b in border(u):
+                if b not in SSET[u[2]]:
+                    scale("v", u, b)
+        elif s[0] == "Y":
             ycopy("v", u)
-    ycopy("v", last)
-    for u in units:
-        for b in border(u):
-            if b in sset(u):
-                scale("s", u, b)
-    for u in pun:
-        ycopy("s", u)
+        else:
+            lo, hi = CH[u[1]]
+            for b in range(G):
+                wait(v, "v", "sz%s_%d" % (tag(u), b), 1)
+            v.quantize_mx(sl("tq%d" % u[0], lo, hi), sl("tz%d" % u[0], lo, hi), sl("tb%d" % u[0], 4 * lo, 4 * hi)).then_inc(T.sem["qt" + tag(u)], 1)
+    for s in SQ:
+        u = unit(s)
+        if s[0] == "Y":
+            ycopy("s", u)
+        else:
+            for b in border(u):
+                if b in SSET[u[2]]:
+                    scale("s", u, b)
 
     n = 0
-    for u in units[:-1] + pun + [last]:
+    for s in ST:
+        u = unit(s)
         lo, hi = CH[u[1]]
         wait(g.sync, "y", "cy" + tag(u), 1)
         g.sync.dma_start(T.y[:, NC * u[0] + lo:NC * u[0] + hi], sl("yb", NC * u[0] + lo, NC * u[0] + hi)).then_inc(T.sem.st, 16)
         n += 16
     g.sync.wait_ge(T.sem.st, n)
 
-    tot = 0
-    for c, (lo, hi) in enumerate(CH):
-        wait(g, "g", "qx%d" % c, 1)
-        for f in (codes("xq%d" % me, lo, hi), sl("xz%d" % me, lo, hi)):
-            g.remote_dma_fused([RemoteDMATransfer(dst_ids=[dst(m) for m in mates], dma_engine_mask=moff, remote_sem=T.sem["ax%d_%d" % (me, c)],
-                                                  srcs=[f], dsts=[f for m in mates]),
-                                RemoteDMATransfer(dst_ids=[dst(partner)], dma_engine_mask=mon_hi, remote_sem=T.sem["ax%d_%d" % (me, c)],
-                                                  srcs=[f], dsts=[f])], local_sem=T.sem.sent)
-            tot += count(moff) + count(mon_hi)
-    for c, (lo, hi) in enumerate(CH):
-        wait(g, "g", "qt%d_%d" % (me, c), 1)
-        for f in (codes("tq%d" % me, lo, hi), sl("tz%d" % me, lo, hi)):
-            g.remote_dma_fused([RemoteDMATransfer(dst_ids=[dst(partner)], dma_engine_mask=mon_hi, remote_sem=T.sem["at%d_%d" % (me, c)], srcs=[f], dsts=[f])],
-                               local_sem=T.sem.sent)
-            tot += count(mon_hi)
-    g.wait_ge(T.sem.sent, tot)
+    tot = [0]
+
+    def send(nm, j, c, to):
+        lo, hi = CH[c]
+        sem = T.sem["a%s%d_%d" % (nm, j, c)]
+        for f in (codes("%sq%d" % (nm, j), lo, hi), sl("%sz%d" % (nm, j), lo, hi)):
+            tr = []
+            for m, js in ((moff, [k for k in mates if k in to]), (mon_hi, [k for k in [partner] if k in to])):
+                if js:
+                    tr.append(RemoteDMATransfer(dst_ids=[dst(k) for k in js], dma_engine_mask=m, remote_sem=sem, srcs=[f], dsts=[f for k in js]))
+                    tot[0] += count(m)
+            g.remote_dma_fused(tr, local_sem=T.sem.sent)
+
+    for s in GQ:
+        c = int(s[-1])
+        if s[0] == "r":
+            wait(g, "g", "a%s%d_%d" % (s[1], role["m"], c), 2 * count(moff))
+            send(s[1], role["m"], c, [partner])
+            continue
+        wait(g, "g", "qx%d" % c if s[0] == "x" else "qt%d_%d" % (me, c), 1)
+        to = [role[r] for r in "pmn" if s[0] == "x" or r + s[1] in SEND]
+        send(s[0], me, c, [k for k in to if not (k == role["n"] and s in RELAY)])
+    g.wait_ge(T.sem.sent, tot[0])

from concourse.bass import DstId, RemoteDMATransfer
from concourse.mybir import dt, AluOpType, ActivationFunctionType

N, NC, G, SCALE = 4, 512, 4, 0.047
CH = [(0, 256), (256, 512)]
NCH = len(CH)
ALOAD = 2
XORDER = [0, 1]
AORDER = [0, 2, 1, 3]
SEND = ["m1", "n1", "p0", "p1"]
RELAY = ["x1"]
GQ = ["x0", "x1", "t1", "t0", "rx1"]
PE = "Zo1 Zo0 Yo1 Yo0 Zm0 Zn0 Yp1 Ym0 Yn0 Yp0 Ym1 Yn1".split()
VQ = "To1 W Qo1 To0 Yo1 Qo0 Yo0 Tm0 Qm0 Tn0 Qn0 Yp1 Yn0 Ym1".split()
SQ = "To1 To0 Tm0 Tn0 Ym0 Yp0 Yn1".split()
ST = "o1 o0 m0 p1 n0 p0 m1 n1".split()
SSET = {"o1": (0, 1, 2), "o0": (0, 1), "m0": (0, 1), "n0": (0, 1)}
BANKS = 8

SCRATCH = {
    "xb": ("sbuf", [128, 4 * NC], "bfloat16"),
    "ab": ("sbuf", [128, 4 * 512], "bfloat16"),
    "wb": ("sbuf", [128, 512], "bfloat16"),
    "bf": ("sbuf", [128, 512], "bfloat16"),
    "aq": ("sbuf", [128, 512], "float8_e4m3fn_x4"),
    "az": ("sbuf", [128, 512], "uint8"),
    "wq": ("sbuf", [128, 128], "float8_e4m3fn_x4"),
    "wz": ("sbuf", [128, 128], "uint8"),
    "bq": ("sbuf", [128, 128], "float8_e4m3fn_x4"),
    "bz": ("sbuf", [128, 128], "uint8"),
    "yb": ("sbuf", [128, N * NC], "float32"),
    "ps": ("psum", [128, 512 * BANKS], "float32"),
}
for _j in range(N):
    SCRATCH["xq%d" % _j] = ("sbuf", [128, NC], "float8_e4m3fn_x4")
    SCRATCH["xz%d" % _j] = ("sbuf", [128, NC], "uint8")
    SCRATCH["tq%d" % _j] = ("sbuf", [128, NC], "float8_e4m3fn_x4")
    SCRATCH["tz%d" % _j] = ("sbuf", [128, NC], "uint8")
    SCRATCH["tb%d" % _j] = ("sbuf", [128, 4 * NC], "bfloat16")
SEMAPHORES = ["lw", "lb", "qw", "qb", "st", "sent"]
for _c in range(NCH):
    SEMAPHORES += ["lx%d" % _c, "qx%d" % _c]
    for _j in range(N):
        SEMAPHORES += ["ax%d_%d" % (_j, _c), "at%d_%d" % (_j, _c), "qt%d_%d" % (_j, _c), "py%d_%d" % (_j, _c), "cy%d_%d" % (_j, _c)]
        for _b in range(G):
            SEMAPHORES += ["pz%d_%d_%d" % (_j, _c, _b), "sz%d_%d_%d" % (_j, _c, _b)]
for _i in range(4):
    SEMAPHORES += ["la%d" % _i, "qa%d" % _i]


def count(mask):
    return bin(mask).count("1")


def rank_program(g, core, T, topo):
    me = T.rank_of(core)
    if me is None:
        return
    here = topo.chip(core)
    others = [j for j in range(N) if j != me]
    partner = [j for j in others if topo.chip(T.cores[j]) == here][0]
    mates = [j for j in others if topo.mates(topo.chip(T.cores[j]), here)]
    mates.sort(key=lambda j: topo.die(T.cores[j]) != topo.die(core))
    role = {"o": me, "p": partner, "m": mates[0], "n": mates[1]}
    moff = topo.mask(core, T.cores[mates[0]])
    mon_hi = topo.mask(core, T.cores[partner]) & ~moff

    seen = set()

    def wait(q, qn, ev, n):
        if (qn, ev) not in seen:
            seen.add((qn, ev))
            q.wait_ge(T.sem[ev], n)

    def sl(name, lo, hi):
        return T[name][:, lo:hi]

    def codes(name, lo, hi):
        return T[name][:, lo:hi].bitcast(dt.uint8)

    def dst(j):
        a = topo.addr(T.cores[j])
        return DstId(rid=a[0], pnc=a[1])

    def unit(s):
        return role[s[-2]], int(s[-1]), s[-2:]

    def tag(u):
        return "%d_%d" % u[:2]

    def landed(nm, u):
        relayed = u[2][0] == "n" and "%s%d" % (nm, u[1]) in RELAY
        return 2 * count(mon_hi if u[0] == partner or relayed else moff)

    def border(u):
        s = [b for b in range(G) if b in SSET[u[2]]]
        v = [b for b in range(G) if b not in SSET[u[2]]]
        o = []
        while s or v:
            if s:
                o.append(s.pop(0))
            if v:
                o.append(v.pop(0))
        return o

    lq = [g.sync, g.scalar]
    k = 0
    for c in XORDER:
        lo, hi = CH[c]
        lq[k % 2].dma_start(sl("xb", 4 * lo, 4 * hi), T.x[:, 4 * lo:4 * hi]).then_inc(T.sem["lx%d" % c], 16)
        k += 1
    w = 2048 // ALOAD
    for i in range(ALOAD):
        lq[k % 2].dma_start(sl("ab", w * i, w * i + w), T.a[:, w * i:w * i + w]).then_inc(T.sem["la%d" % i], 16)
        k += 1
    lq[k % 2].dma_start(T.wb[:], T.w[:]).then_inc(T.sem.lw, 16)
    lq[(k + 1) % 2].dma_start(T.bf[:], T.bb[:]).then_inc(T.sem.lb, 16)

    pe = g.tensor
    bank_of, rel = {}, {}
    turn = [0]

    def bank():
        b = turn[0] % BANKS
        turn[0] += 1
        if b in rel:
            wait(pe, "pe", rel[b], 1)
        return b

    def xwait(u):
        if u[0] == me:
            wait(pe, "pe", "qx%d" % u[1], 1)
        else:
            wait(pe, "pe", "ax" + tag(u), landed("x", u))

    for s in PE:
        u = unit(s)
        lo, hi = CH[u[1]]
        x, xz = sl("xq%d" % u[0], lo, hi), sl("xz%d" % u[0], lo, hi)
        if s[0] == "Z":
            for b in border(u):
                k = bank()
                xwait(u)
                wait(pe, "pe", "qa%d" % b, 1)
                pe.matmul_mx(sl("ps", 512 * k, 512 * k + hi - lo), sl("aq", 128 * b, 128 * b + 128), sl("az", 128 * b, 128 * b + 128),
                             x, xz, True, True).then_inc(T.sem["pz%s_%d" % (tag(u), b)], 1)
                rel[k] = "sz%s_%d" % (tag(u), b)
                bank_of[u, b] = k
        else:
            k = bank()
            xwait(u)
            wait(pe, "pe", "qw", 1)
            o = sl("ps", 512 * k, 512 * k + hi - lo)
            pe.matmul_mx(o, T.wq[:], T.wz[:], x, xz, True, False)
            wait(pe, "pe", "qb", 1)
            if u[2] in SEND:
                wait(pe, "pe", "at" + tag(u), landed("t", u))
            else:
                wait(pe, "pe", "qt" + tag(u), 1)
            pe.matmul_mx(o, T.bq[:], T.bz[:], sl("tq%d" % u[0], lo, hi), sl("tz%d" % u[0], lo, hi), False, True).then_inc(T.sem["py" + tag(u)], 1)
            rel[k] = "cy" + tag(u)
            bank_of[u] = k

    def scale(qn, u, b):
        q = g.scalar if qn == "s" else g.vector
        lo, hi = CH[u[1]]
        k = bank_of[u, b]
        wait(q, qn, "pz%s_%d" % (tag(u), b), 1)
        o = T["tb%d" % u[0]][:, 4 * lo + b:4 * hi:4]
        i = sl("ps", 512 * k, 512 * k + hi - lo)
        if qn == "s":
            r = q.activation(o, i, ActivationFunctionType.Copy, scale=SCALE)
        else:
            r = q.tensor_scalar(o, i, SCALE, None, AluOpType.mult)
        r.then_inc(T.sem["sz%s_%d" % (tag(u), b)], 1)

    def ycopy(qn, u):
        q = g.scalar if qn == "s" else g.vector
        lo, hi = CH[u[1]]
        k = bank_of[u]
        wait(q, qn, "py" + tag(u), 1)
        o = sl("yb", NC * u[0] + lo, NC * u[0] + hi)
        i = sl("ps", 512 * k, 512 * k + hi - lo)
        r = q.activation(o, i, ActivationFunctionType.Copy) if qn == "s" else q.tensor_copy(o, i)
        r.then_inc(T.sem["cy" + tag(u)], 1)

    v = g.vector
    for c in XORDER:
        lo, hi = CH[c]
        wait(v, "v", "lx%d" % c, 16)
        v.quantize_mx(sl("xq%d" % me, lo, hi), sl("xz%d" % me, lo, hi), sl("xb", 4 * lo, 4 * hi)).then_inc(T.sem["qx%d" % c], 1)
    for i in border(unit(PE[0])):
        wait(v, "v", "la%d" % (i * ALOAD // 4), 16)
        v.quantize_mx(sl("aq", 128 * i, 128 * i + 128), sl("az", 128 * i, 128 * i + 128), sl("ab", 512 * i, 512 * i + 512)).then_inc(T.sem["qa%d" % i], 1)

    for s in VQ:
        if s == "W":
            for nm, src, ld in (("w", "wb", "lw"), ("b", "bf", "lb")):
                wait(v, "v", ld, 16)
                v.quantize_mx(T[nm + "q"][:], T[nm + "z"][:], T[src][:]).then_inc(T.sem["q" + nm], 1)
            continue
        u = unit(s)
        if s[0] == "T":
            for b in border(u):
                if b not in SSET[u[2]]:
                    scale("v", u, b)
        elif s[0] == "Y":
            ycopy("v", u)
        else:
            lo, hi = CH[u[1]]
            for b in range(G):
                wait(v, "v", "sz%s_%d" % (tag(u), b), 1)
            v.quantize_mx(sl("tq%d" % u[0], lo, hi), sl("tz%d" % u[0], lo, hi), sl("tb%d" % u[0], 4 * lo, 4 * hi)).then_inc(T.sem["qt" + tag(u)], 1)
    for s in SQ:
        u = unit(s)
        if s[0] == "Y":
            ycopy("s", u)
        else:
            for b in border(u):
                if b in SSET[u[2]]:
                    scale("s", u, b)

    n = 0
    for s in ST:
        u = unit(s)
        lo, hi = CH[u[1]]
        wait(g.sync, "y", "cy" + tag(u), 1)
        g.sync.dma_start(T.y[:, NC * u[0] + lo:NC * u[0] + hi], sl("yb", NC * u[0] + lo, NC * u[0] + hi)).then_inc(T.sem.st, 16)
        n += 16
    g.sync.wait_ge(T.sem.st, n)

    tot = [0]

    def send(nm, j, c, to):
        lo, hi = CH[c]
        sem = T.sem["a%s%d_%d" % (nm, j, c)]
        for f in (codes("%sq%d" % (nm, j), lo, hi), sl("%sz%d" % (nm, j), lo, hi)):
            tr = []
            for m, js in ((moff, [k for k in mates if k in to]), (mon_hi, [k for k in [partner] if k in to])):
                if js:
                    tr.append(RemoteDMATransfer(dst_ids=[dst(k) for k in js], dma_engine_mask=m, remote_sem=sem, srcs=[f], dsts=[f for k in js]))
                    tot[0] += count(m)
            g.remote_dma_fused(tr, local_sem=T.sem.sent)

    for s in GQ:
        c = int(s[-1])
        if s[0] == "r":
            wait(g, "g", "a%s%d_%d" % (s[1], role["m"], c), 2 * count(moff))
            send(s[1], role["m"], c, [partner])
            continue
        wait(g, "g", "qx%d" % c if s[0] == "x" else "qt%d_%d" % (me, c), 1)
        to = [role[r] for r in "pmn" if s[0] == "x" or r + s[1] in SEND]
        send(s[0], me, c, [k for k in to if not (k == role["n"] and s in RELAY)])
    g.wait_ge(T.sem.sent, tot[0])
